import numpy as np
import ml_dtypes


def mxq(x, axis, fmt="e4m3"):
    dtype, down = {"e4m3": (ml_dtypes.float8_e4m3fn, 7), "e5m2": (ml_dtypes.float8_e5m2, 14)}[fmt]
    v = np.moveaxis(np.asarray(x, np.float32).astype(ml_dtypes.bfloat16).astype(np.float64), axis, -1)
    blocks = v.reshape(v.shape[:-1] + (-1, 32))
    amax = np.abs(blocks).max(-1, keepdims=True)
    byte = np.maximum(np.where(amax > 0, np.frexp(amax)[1] - 1 + 127, 0) - down, 1)
    scale = np.exp2(byte - 127.0)
    codes = (blocks / scale).astype(np.float32).astype(dtype).astype(np.float64)
    return np.moveaxis((codes * scale).reshape(v.shape), -1, axis)


WIDE = False


def mx_kscale(k):
    if not WIDE:
        return np.ones(k)
    levels = np.array([10, -10, 5, -5, 0])
    if k % 512:
        return np.exp2(np.random.permutation(np.resize(levels, k // 32))).repeat(32)
    a = np.empty((k // 512, 16))
    for p in range(k // 512):
        a[p, :8] = np.random.permutation(np.resize(levels, 8))
        for g in range(8):
            far = levels[np.abs(levels - a[p, g]) >= 10]
            a[p, g + 8] = far[np.random.randint(len(far))]
    return np.exp2(a.ravel()).repeat(32)


def f64(x):
    return np.asarray(x).astype(np.float64)


def striped(idx):
    return np.tile(idx.reshape(-1, 16).T, (8, 1)).astype(np.uint16)


def unstriped(offs):
    return offs[:16].T.reshape(-1).astype(np.int64)


E2M1 = np.array([0.0, 0.5, 1.0, 1.5, 2.0, 3.0, 4.0, 6.0, -0.0, -0.5, -1.0, -1.5, -2.0, -3.0, -4.0, -6.0])


def pack_weight(w, fmt):
    k, n = w.shape
    w = f64(np.asarray(w, np.float32).astype(ml_dtypes.bfloat16)).reshape(k // 32, 32, n)
    amax = np.abs(w).max(1)
    if fmt == "e4m3":
        byte = np.frexp(amax)[1] - 1 + 127 - 7
    else:
        mant, ex = np.frexp(amax / 6.0)
        byte = np.where(mant > 0.5, ex, ex - 1) + 127
    byte = np.clip(np.where(amax > 0, byte, 1), 1, 254)
    scaled = (w * np.exp2(127.0 - byte)[:, None, :]).reshape(k, n).astype(np.float32)
    by_word = np.ascontiguousarray(scaled.reshape(k // 512, 128, 4, n).transpose(0, 1, 3, 2))
    if fmt == "e4m3":
        words = by_word.astype(ml_dtypes.float8_e4m3fn).view(np.uint8)
    else:
        c = by_word.astype(ml_dtypes.float4_e2m1fn).view(np.uint8) & 0xF
        words = (c[..., 0::2] | (c[..., 1::2] << 4)).reshape(k // 512, 128, 2 * n)
    return np.ascontiguousarray(words), np.ascontiguousarray(byte.astype(np.uint8).reshape(k // 512, 16, n))


def unpack_weight(words, scales, fmt):
    g, _, n = scales.shape
    words = np.ascontiguousarray(words).reshape(g, 128, n, -1)
    if fmt == "e4m3":
        vals = words.view(ml_dtypes.float8_e4m3fn).astype(np.float64)
    else:
        nib = np.empty((g, 128, n, 4), np.uint8)
        nib[..., 0::2] = words & 0xF
        nib[..., 1::2] = words >> 4
        vals = E2M1[nib]
    vals = vals * np.repeat(np.exp2(scales.astype(np.float64) - 127.0), 8, axis=1)[..., None]
    return vals.transpose(0, 1, 3, 2).reshape(g * 512, n)


def gelu(v):
    return 0.5 * v * (1.0 + np.tanh(np.sqrt(2.0 / np.pi) * (v + 0.044715 * v**3)))


K, T, E, C, H, N = 512, 512, 4, 256, 512, 128


def by_expert(wq, xq):
    return np.concatenate([wq[e].T @ xq[:, e * C:(e + 1) * C] for e in range(E)], axis=1)


def setup_inputs():
    n = np.random.standard_normal
    s = mx_kscale(K)[:, None]
    u = mx_kscale(H)
    first = np.random.permutation(np.repeat(np.arange(E), T // E))
    second = (first + 1 + np.random.permutation(np.repeat(np.arange(E - 1), -(-T // (E - 1)))[:T])) % E
    while np.bincount(second, minlength=E).max() != T // E:
        load = np.bincount(second, minlength=E); hi, lo = int(load.argmax()), int(load.argmin())
        t = np.flatnonzero((second == hi) & (first != lo))[0]; second[t] = lo
    slot_token = np.empty(E * C, np.int64); pos = np.empty((2, T), np.int64); fill = np.zeros(E, np.int64)
    place = np.stack([np.random.permutation(C) for _ in range(E)])
    for r, deal in enumerate((first, second)):
        for t in np.random.permutation(T):
            e = deal[t]; j = e * C + place[e, fill[e]]; fill[e] += 1; slot_token[j] = t; pos[r, t] = j
    g = np.random.uniform(0.2, 0.8, T)
    w1 = [pack_weight(m, "e2m1") for m in n((E, K, H)) / np.sqrt(K) / s[None]]
    w3 = [pack_weight(m, "e2m1") for m in n((E, K, H)) / np.sqrt(K) / s[None] * u[None, None, :]]
    w2 = [pack_weight(m, "e2m1") for m in n((E, H, N)) / np.sqrt(H) / u[None, :, None]]
    x = pack_weight(n((K, T)) * s, "e4m3")
    return {
        "x_words": x[0],
        "x_scales": x[1],
        "w1_words": np.stack([m[0] for m in w1]),
        "w1_scales": np.stack([m[1] for m in w1]),
        "w3_words": np.stack([m[0] for m in w3]),
        "w3_scales": np.stack([m[1] for m in w3]),
        "w2_words": np.stack([m[0] for m in w2]),
        "w2_scales": np.stack([m[1] for m in w2]),
        "gate": np.stack([np.tile(g, (N, 1)), np.tile(1.0 - g, (N, 1))]).astype(np.float32),
        "offs": striped(slot_token),
        "pos1": striped(pos[0]),
        "pos2": striped(pos[1]),
    }


def reference(x_words, x_scales, w1_words, w1_scales, w3_words, w3_scales, w2_words, w2_scales, gate, offs, pos1, pos2):
    idx = unstriped(offs)
    w1 = np.stack([unpack_weight(w1_words[e], w1_scales[e], "e2m1") for e in range(E)])
    w3 = np.stack([unpack_weight(w3_words[e], w3_scales[e], "e2m1") for e in range(E)])
    w2 = np.stack([unpack_weight(w2_words[e], w2_scales[e], "e2m1") for e in range(E)])
    xq = unpack_weight(x_words, x_scales, "e4m3")[:, idx]
    h = gelu(by_expert(w1, xq))
    h = h * by_expert(w3, xq)
    y = by_expert(w2, mxq(h, 0, "e4m3"))
    return f64(gate[0]) * y[:, unstriped(pos1)] + f64(gate[1]) * y[:, unstriped(pos2)]

@@ -1,0 +1,194 @@
+from contextlib import ExitStack
+
+import concourse.mybir as mybir
+from concourse.masks import make_identity
+
+K, T, E, C, H, N = 512, 512, 4, 256, 512, 128
+P = 128
+FLOPS = 2 * E * C * (2 * K * H + H * N)
+
+F32 = mybir.dt.float32
+BF16 = mybir.dt.bfloat16
+I32 = mybir.dt.int32
+U32 = mybir.dt.uint32
+U16 = mybir.dt.uint16
+U8 = mybir.dt.uint8
+FP8X4 = mybir.dt.float8_e4m3fn_x4
+FP4X4 = mybir.dt.float4_e2m1fn_x4
+MULT = mybir.AluOpType.mult
+ADD = mybir.AluOpType.add
+GELU = mybir.ActivationFunctionType.Gelu_apprx_tanh
+
+
+def tile_moe_pkd_glu_gelu_kernel(
+    tc, x_words, x_scales, w1_words, w1_scales, w3_words, w3_scales, w2_words, w2_scales, gate, offs, pos1, pos2, out
+):
+    nc = tc.nc
+    with ExitStack() as ctx:
+        keep = ctx.enter_context(tc.tile_pool(name="keep", bufs=1))
+        work = ctx.enter_context(tc.tile_pool(name="work", bufs=8))
+        psum = ctx.enter_context(tc.psum_pool(name="psum", bufs=1))
+
+        offs_sb = keep.tile([P, E * C // 16], U16, name="offs_sb")
+        pos1_sb = keep.tile([P, T // 16], U16, name="pos1_sb")
+        pos2_sb = keep.tile([P, T // 16], U16, name="pos2_sb")
+        xw = keep.tile([P, T], U32, name="xw", align_bytes=64)
+        xs = keep.tile([P, T], U8, name="xs", align_bytes=64)
+        w1w = keep.tile([P, E, 2 * H], U8, name="w1w", align_bytes=64)
+        w3w = keep.tile([P, E, 2 * H], U8, name="w3w", align_bytes=64)
+        w2w = keep.tile([P, E, 2 * N], U8, name="w2w", align_bytes=64)
+        w1s = keep.tile([P, E, H], U8, name="w1s", align_bytes=64)
+        w3s = keep.tile([P, E, H], U8, name="w3s", align_bytes=64)
+        w2s = keep.tile([P, E, N], U8, name="w2s", align_bytes=64)
+        gate_sb = keep.tile([P, 2, T], F32, name="gate_sb", align_bytes=64)
+        ident = keep.tile([P, P], F32, name="ident", align_bytes=64)
+        ys = keep.tile([P, E * C], F32, name="ys", align_bytes=64)
+
+        nc.vector.memset(xs[:].bitcast(I32), 0)
+        for plane in (w1s, w3s, w2s):
+            nc.vector.memset(plane[:].rearrange("p e n -> p (e n)").bitcast(I32), 0)
+        nc.vector.memset(ident[:], 0.0)
+        make_identity(nc, ident[:], nomemset=True)
+
+        def load_words(queue, dst, src, e0, e1):
+            queue.dma_start(dst[:, e0:e1, :].bitcast(I32), src[e0:e1, 0].rearrange("e p n -> p e n").bitcast(I32))
+
+        def load_scales(queue, dst, src):
+            for q in range(4):
+                queue.dma_start(
+                    dst[32 * q : 32 * q + 4, :, :].bitcast(I32),
+                    src[:, 0, 4 * q : 4 * q + 4, :].rearrange("e r n -> r e n").bitcast(I32),
+                )
+
+        nc.sync.dma_start(offs_sb[:], offs)
+        nc.sync.dma_start(xw[:].bitcast(I32), x_words[0].rearrange("p t r -> p (t r)").bitcast(I32))
+        for q in range(4):
+            nc.scalar.dma_start(xs[32 * q : 32 * q + 4, :].bitcast(I32), x_scales[0, 4 * q : 4 * q + 4, :].bitcast(I32))
+        load_words(nc.sync, w1w, w1_words, 0, 4)
+        load_scales(nc.sync, w1s, w1_scales)
+        load_words(nc.sync, w3w, w3_words, 0, 4)
+        load_scales(nc.sync, w3s, w3_scales)
+        load_words(nc.sync, w2w, w2_words, 0, 4)
+        load_scales(nc.sync, w2s, w2_scales)
+        nc.sync.dma_start(pos1_sb[:], pos1)
+        nc.sync.dma_start(pos2_sb[:], pos2)
+        nc.sync.dma_start(gate_sb[:], gate.rearrange("g n t -> n g t"))
+
+        gw = [keep.tile([P, C], U32, name="gw%d" % e, align_bytes=64) for e in range(E)]
+        gs = [keep.tile([P, C], U8, name="gs%d" % e, align_bytes=64) for e in range(E)]
+
+        def gather(e):
+            picks = offs_sb[:, e * C // 16 : (e + 1) * C // 16]
+            nc.vector.tensor_copy(gw[e][:], xw[:].indirect(picks))
+            nc.vector.tensor_copy(gs[e][:], xs[:].indirect(picks))
+
+        gelus, hs, hTs = {}, {}, {}
+
+        def product(acc, j, ww, ws):
+            e, cols = j // 2, slice((j % 2) * P, (j % 2 + 1) * P)
+            nc.tensor.matmul_mx(
+                out=acc[:],
+                lhsT=gw[e][:, cols].bitcast(FP8X4),
+                lhsT_scale=gs[e][:, cols],
+                rhs=ww[:, e, :].bitcast(FP4X4),
+                rhs_scale=ws[:, e, :],
+                start=True,
+                stop=True,
+            )
+
+        def gelu_side(j):
+            a = psum.tile([P, H], F32, name="a", tag="ring", bufs=5)
+            product(a, j, w1w, w1s)
+            g = work.tile([P, H], F32, name="g", align_bytes=64)
+            nc.scalar.activation(
+                g[:].rearrange("s (u p d) -> s u p d", u=2, d=2), a[:].rearrange("s (p u d) -> s u p d", u=2, d=2), GELU
+            )
+            gelus[j] = g
+
+        def linear_side(j):
+            if j < 3:
+                b = psum.tile([P, H], F32, name="b", tag="side", bufs=3)
+            else:
+                b = psum.tile([P, H], F32, name="b", tag="ring", bufs=5)
+            product(b, j, w3w, w3s)
+            h = work.tile([P, H], BF16, name="h", align_bytes=64)
+            nc.vector.tensor_tensor(
+                h[:].rearrange("s (u p d) -> s u p d", u=2, d=2),
+                b[:].rearrange("s (p u d) -> s u p d", u=2, d=2),
+                gelus[j][:].rearrange("s (u p d) -> s u p d", u=2, d=2),
+                MULT,
+            )
+            hs[j] = h
+
+        def turn(tiles):
+            width = P * len(tiles)
+            turned = psum.tile([P, 2, width], F32, name="turned", tag="ring", bufs=5)
+            for n, j in enumerate(tiles):
+                words = hs[j][:].bitcast(F32)
+                for u in range(2):
+                    nc.tensor.transpose(turned[:, u, n * P : (n + 1) * P], words[:, u * P : (u + 1) * P], ident[:])
+            hT = work.tile([P, 4 * width], BF16, name="hT", align_bytes=64)
+            nc.scalar.copy(hT[:].bitcast(F32).rearrange("p (s u) -> p s u", u=2), turned[:].rearrange("p u s -> p s u"))
+            hTs[tiles] = hT
+
+        def second_layer(tiles):
+            width = P * len(tiles)
+            e = tiles[0] // 2
+            hq = work.tile([P, width], U32, name="hq", align_bytes=64)
+            hqs = work.tile([P, width], U8, name="hqs", align_bytes=64)
+            nc.vector.quantize_mx(out=hq[:].bitcast(FP8X4), scales=hqs[:], in_=hTs[tiles][:])
+            y = psum.tile([P, width], F32, name="y", tag="side", bufs=3)
+            nc.tensor.matmul_mx(
+                out=y[:],
+                lhsT=w2w[:, e, :].bitcast(FP4X4),
+                lhsT_scale=w2s[:, e, :],
+                rhs=hq[:].bitcast(FP8X4),
+                rhs_scale=hqs[:],
+                start=True,
+                stop=True,
+            )
+            nc.scalar.copy(ys[:, tiles[0] * P : tiles[0] * P + width], y[:])
+
+        for e in range(E):
+            gather(e)
+        for j in range(8):
+            gelu_side(j)
+        for j in range(4):
+            linear_side(j)
+        turn((0, 1))
+        linear_side(4)
+        linear_side(5)
+        turn((2, 3))
+        linear_side(6)
+        linear_side(7)
+        turn((4, 5))
+        turn((6,))
+        turn((7,))
+        for tiles in ((0, 1), (2, 3), (4, 5), (6,), (7,)):
+            second_layer(tiles)
+
+        pieces = ((0, 256), (256, 384), (384, 512))
+        parts = {}
+
+        def fetch(n, r):
+            t0, t1 = pieces[n]
+            part = keep.tile([P, t1 - t0], F32, name="part%d_%d" % (n, r), align_bytes=64)
+            picks = (pos1_sb, pos2_sb)[r][:, t0 // 16 : t1 // 16]
+            nc.vector.tensor_tensor(part[:], ys[:].indirect(picks), gate_sb[:, r, t0:t1], MULT)
+            parts[n, r] = part
+
+        def finish(n):
+            t0, t1 = pieces[n]
+            res = keep.tile([P, t1 - t0], F32, name="res%d" % n, align_bytes=64)
+            nc.vector.tensor_tensor(res[:], parts[n, 0][:], parts[n, 1][:], ADD)
+            nc.sync.dma_start(out[:, t0:t1], res[:])
+
+        fetch(0, 0)
+        fetch(0, 1)
+        fetch(1, 0)
+        finish(0)
+        fetch(1, 1)
+        fetch(2, 0)
+        fetch(2, 1)
+        finish(1)
+        finish(2)

@@ -32,55 +32,56 @@ def tile_moe_pkd_glu_gelu_kernel(
         offs_sb = keep.tile([P, E * C // 16], U16, name="offs_sb")
         pos1_sb = keep.tile([P, T // 16], U16, name="pos1_sb")
         pos2_sb = keep.tile([P, T // 16], U16, name="pos2_sb")
-        xw = keep.tile([P, T], U32, name="xw", align_bytes=64)
-        xs = keep.tile([P, T], U8, name="xs", align_bytes=64)
+        xw = keep.tile([P, T], U32, name="xw", tag="early_words", align_bytes=64)
+        xs = keep.tile([P, T], U8, name="xs", tag="early_scales", align_bytes=64)
         w1w = keep.tile([P, E, 2 * H], U8, name="w1w", align_bytes=64)
         w3w = keep.tile([P, E, 2 * H], U8, name="w3w", align_bytes=64)
-        w2w = keep.tile([P, E, 2 * N], U8, name="w2w", align_bytes=64)
         w1s = keep.tile([P, E, H], U8, name="w1s", align_bytes=64)
         w3s = keep.tile([P, E, H], U8, name="w3s", align_bytes=64)
         w2s = keep.tile([P, E, N], U8, name="w2s", align_bytes=64)
-        gate_sb = keep.tile([P, 2, T], F32, name="gate_sb", align_bytes=64)
         ident = keep.tile([P, P], F32, name="ident", align_bytes=64)
         ys = keep.tile([P, E * C], F32, name="ys", align_bytes=64)
 
-        nc.vector.memset(xs[:].bitcast(I32), 0)
-        for plane in (w1s, w3s, w2s):
-            nc.vector.memset(plane[:].rearrange("p e n -> p (e n)").bitcast(I32), 0)
+        nc.gpsimd.memset(w1s[:].rearrange("p e n -> p (e n)").bitcast(I32), 0)
         nc.vector.memset(ident[:], 0.0)
         make_identity(nc, ident[:], nomemset=True)
+        for plane in (w3s, w2s):
+            nc.vector.memset(plane[:].rearrange("p e n -> p (e n)").bitcast(I32), 0)
 
         def load_words(queue, dst, src, e0, e1):
             queue.dma_start(dst[:, e0:e1, :].bitcast(I32), src[e0:e1, 0].rearrange("e p n -> p e n").bitcast(I32))
 
-        def load_scales(queue, dst, src):
-            for q in range(4):
+        def load_scales(queue, dst, src, quadrants):
+            for q in quadrants:
                 queue.dma_start(
                     dst[32 * q : 32 * q + 4, :, :].bitcast(I32),
                     src[:, 0, 4 * q : 4 * q + 4, :].rearrange("e r n -> r e n").bitcast(I32),
                 )
 
         nc.sync.dma_start(offs_sb[:], offs)
-        nc.sync.dma_start(xw[:].bitcast(I32), x_words[0].rearrange("p t r -> p (t r)").bitcast(I32))
         for q in range(4):
-            nc.scalar.dma_start(xs[32 * q : 32 * q + 4, :].bitcast(I32), x_scales[0, 4 * q : 4 * q + 4, :].bitcast(I32))
-        load_words(nc.sync, w1w, w1_words, 0, 4)
-        load_scales(nc.sync, w1s, w1_scales)
-        load_words(nc.sync, w3w, w3_words, 0, 4)
-        load_scales(nc.sync, w3s, w3_scales)
-        load_words(nc.sync, w2w, w2_words, 0, 4)
-        load_scales(nc.sync, w2s, w2_scales)
+            rows = x_scales[0, 4 * q : 4 * q + 4, :].bitcast(I32)
+            queue = nc.sync if q < 2 else nc.scalar
+            queue.dma_start(xs[32 * q : 32 * q + 32, :].bitcast(I32), rows.unsqueeze(0).to_broadcast([8, 4, T // 4]))
+        nc.scalar.dma_start(xw[:].bitcast(I32), x_words[0].rearrange("p t r -> p (t r)").bitcast(I32))
+        load_words(nc.sync, w1w, w1_words, 0, 2)
+        load_scales(nc.scalar, w1s, w1_scales, (0,))
+        load_scales(nc.sync, w1s, w1_scales, (1, 2, 3))
+        load_words(nc.sync, w3w, w3_words, 0, 2)
+        load_scales(nc.sync, w3s, w3_scales, range(4))
+        load_words(nc.sync, w1w, w1_words, 2, 4)
+        load_words(nc.sync, w3w, w3_words, 2, 4)
         nc.sync.dma_start(pos1_sb[:], pos1)
         nc.sync.dma_start(pos2_sb[:], pos2)
-        nc.sync.dma_start(gate_sb[:], gate.rearrange("g n t -> n g t"))
+        load_scales(nc.sync, w2s, w2_scales, range(4))
 
         gw = [keep.tile([P, C], U32, name="gw%d" % e, align_bytes=64) for e in range(E)]
         gs = [keep.tile([P, C], U8, name="gs%d" % e, align_bytes=64) for e in range(E)]
 
         def gather(e):
             picks = offs_sb[:, e * C // 16 : (e + 1) * C // 16]
-            nc.vector.tensor_copy(gw[e][:], xw[:].indirect(picks))
             nc.vector.tensor_copy(gs[e][:], xs[:].indirect(picks))
+            nc.vector.tensor_copy(gw[e][:], xw[:].indirect(picks))
 
         gelus, hs, hTs = {}, {}, {}
 
@@ -99,7 +100,10 @@ def tile_moe_pkd_glu_gelu_kernel(
         def gelu_side(j):
             a = psum.tile([P, H], F32, name="a", tag="ring", bufs=5)
             product(a, j, w1w, w1s)
-            g = work.tile([P, H], F32, name="g", align_bytes=64)
+            if j < 7:
+                g = work.tile([P, H], F32, name="g", align_bytes=64)
+            else:
+                g = keep.tile([P, H], F32, name="g_last", tag="last", align_bytes=64)
             nc.scalar.activation(
                 g[:].rearrange("s (u p d) -> s u p d", u=2, d=2), a[:].rearrange("s (p u d) -> s u p d", u=2, d=2), GELU
             )
@@ -134,23 +138,33 @@ def tile_moe_pkd_glu_gelu_kernel(
         def second_layer(tiles):
             width = P * len(tiles)
             e = tiles[0] // 2
-            hq = work.tile([P, width], U32, name="hq", align_bytes=64)
+            hq = hq_all[:, tiles[0] * P : tiles[0] * P + width]
             hqs = work.tile([P, width], U8, name="hqs", align_bytes=64)
-            nc.vector.quantize_mx(out=hq[:].bitcast(FP8X4), scales=hqs[:], in_=hTs[tiles][:])
-            y = psum.tile([P, width], F32, name="y", tag="side", bufs=3)
+            nc.vector.quantize_mx(out=hq.bitcast(FP8X4), scales=hqs[:], in_=hTs[tiles][:])
+            if len(tiles) == 2:
+                y = psum.tile([P, width], F32, name="y", tag="side", bufs=3)
+            else:
+                y = psum.tile([P, width], F32, name="y", tag="ring", bufs=5)
             nc.tensor.matmul_mx(
                 out=y[:],
                 lhsT=w2w[:, e, :].bitcast(FP4X4),
                 lhsT_scale=w2s[:, e, :],
-                rhs=hq[:].bitcast(FP8X4),
+                rhs=hq.bitcast(FP8X4),
                 rhs_scale=hqs[:],
                 start=True,
                 stop=True,
             )
-            nc.scalar.copy(ys[:, tiles[0] * P : tiles[0] * P + width], y[:])
+            if len(tiles) == 2:
+                nc.scalar.copy(ys[:, tiles[0] * P : tiles[0] * P + width], y[:])
+            else:
+                nc.vector.tensor_copy(ys[:, tiles[0] * P : tiles[0] * P + width], y[:])
 
         for e in range(E):
             gather(e)
+        w2w = keep.tile([P, E, 2 * N], U8, name="w2w", tag="early_scales", align_bytes=64)
+        load_words(nc.sync, w2w, w2_words, 0, 4)
+        gate_sb = keep.tile([P, 2, T], F32, name="gate_sb", tag="early_words", align_bytes=64)
+        nc.sync.dma_start(gate_sb[:], gate.rearrange("g n t -> n g t"))
         for j in range(8):
             gelu_side(j)
         for j in range(4):
@@ -164,31 +178,18 @@ def tile_moe_pkd_glu_gelu_kernel(
         turn((4, 5))
         turn((6,))
         turn((7,))
+        hq_all = keep.tile([P, E * C], U32, name="hq_all", tag="last", align_bytes=64)
         for tiles in ((0, 1), (2, 3), (4, 5), (6,), (7,)):
             second_layer(tiles)
 
-        pieces = ((0, 256), (256, 384), (384, 512))
-        parts = {}
-
-        def fetch(n, r):
-            t0, t1 = pieces[n]
-            part = keep.tile([P, t1 - t0], F32, name="part%d_%d" % (n, r), align_bytes=64)
-            picks = (pos1_sb, pos2_sb)[r][:, t0 // 16 : t1 // 16]
-            nc.vector.tensor_tensor(part[:], ys[:].indirect(picks), gate_sb[:, r, t0:t1], MULT)
-            parts[n, r] = part
-
-        def finish(n):
-            t0, t1 = pieces[n]
-            res = keep.tile([P, t1 - t0], F32, name="res%d" % n, align_bytes=64)
-            nc.vector.tensor_tensor(res[:], parts[n, 0][:], parts[n, 1][:], ADD)
-            nc.sync.dma_start(out[:, t0:t1], res[:])
-
-        fetch(0, 0)
-        fetch(0, 1)
-        fetch(1, 0)
-        finish(0)
-        fetch(1, 1)
-        fetch(2, 0)
-        fetch(2, 1)
-        finish(1)
-        finish(2)
+        first = keep.tile([P, T], F32, name="first", align_bytes=64)
+        second = keep.tile([P, T], F32, name="second", align_bytes=64)
+        res = keep.tile([P, T], F32, name="res", align_bytes=64)
+        halves = (slice(0, T // 2), slice(T // 2, T))
+        nc.vector.tensor_tensor(first[:], ys[:].indirect(pos1_sb[:]), gate_sb[:, 0, :], MULT)
+        for half in halves:
+            picks = pos2_sb[:, half.start // 16 : half.stop // 16]
+            nc.vector.tensor_tensor(second[:, half], ys[:].indirect(picks), gate_sb[:, 1, half], MULT)
+        for half in halves:
+            nc.vector.tensor_tensor(res[:, half], first[:, half], second[:, half], ADD)
+            nc.sync.dma_start(out[:, half], res[:, half])

@@ -36,12 +36,14 @@ def tile_moe_pkd_glu_gelu_kernel(
         xs = keep.tile([P, T], U8, name="xs", tag="early_scales", align_bytes=64)
         w1w = keep.tile([P, E, 2 * H], U8, name="w1w", align_bytes=64)
         w3w = keep.tile([P, E, 2 * H], U8, name="w3w", align_bytes=64)
-        w1s = keep.tile([P, E, H], U8, name="w1s", align_bytes=64)
+        w1s_first = keep.tile([P, H], U8, name="w1s_first", align_bytes=64)
+        w1s = keep.tile([P, E - 1, H], U8, name="w1s", align_bytes=64)
         w3s = keep.tile([P, E, H], U8, name="w3s", align_bytes=64)
         w2s = keep.tile([P, E, N], U8, name="w2s", align_bytes=64)
         ident = keep.tile([P, P], F32, name="ident", align_bytes=64)
         ys = keep.tile([P, E * C], F32, name="ys", align_bytes=64)
 
+        nc.gpsimd.memset(w1s_first[96:, :].bitcast(I32), 0)
         nc.gpsimd.memset(w1s[:].rearrange("p e n -> p (e n)").bitcast(I32), 0)
         nc.vector.memset(ident[:], 0.0)
         make_identity(nc, ident[:], nomemset=True)
@@ -65,8 +67,9 @@ def tile_moe_pkd_glu_gelu_kernel(
             queue.dma_start(xs[32 * q : 32 * q + 32, :].bitcast(I32), rows.unsqueeze(0).to_broadcast([8, 4, T // 4]))
         nc.scalar.dma_start(xw[:].bitcast(I32), x_words[0].rearrange("p t r -> p (t r)").bitcast(I32))
         load_words(nc.sync, w1w, w1_words, 0, 2)
-        load_scales(nc.scalar, w1s, w1_scales, (0,))
-        load_scales(nc.sync, w1s, w1_scales, (1, 2, 3))
+        wrapped = w1_scales.rearrange("e s r n -> (e s r) n")[0:28, :].bitcast(I32)
+        nc.scalar.dma_start(w1s_first[0:112, :].bitcast(I32), wrapped.unsqueeze(0).to_broadcast([4, 28, H // 4]))
+        load_scales(nc.sync, w1s, w1_scales[1:], range(4))
         load_words(nc.sync, w3w, w3_words, 0, 2)
         load_scales(nc.sync, w3s, w3_scales, range(4))
         load_words(nc.sync, w1w, w1_words, 2, 4)
@@ -78,10 +81,10 @@ def tile_moe_pkd_glu_gelu_kernel(
         gw = [keep.tile([P, C], U32, name="gw%d" % e, align_bytes=64) for e in range(E)]
         gs = [keep.tile([P, C], U8, name="gs%d" % e, align_bytes=64) for e in range(E)]
 
-        def gather(e):
-            picks = offs_sb[:, e * C // 16 : (e + 1) * C // 16]
-            nc.vector.tensor_copy(gs[e][:], xs[:].indirect(picks))
-            nc.vector.tensor_copy(gw[e][:], xw[:].indirect(picks))
+        def gather(e, first, count):
+            picks = offs_sb[:, (e * C + first) // 16 : (e * C + first + count) // 16]
+            nc.vector.tensor_copy(gs[e][:, first : first + count], xs[:].indirect(picks))
+            nc.vector.tensor_copy(gw[e][:, first : first + count], xw[:].indirect(picks))
 
         gelus, hs, hTs = {}, {}, {}
 
@@ -92,14 +95,14 @@ def tile_moe_pkd_glu_gelu_kernel(
                 lhsT=gw[e][:, cols].bitcast(FP8X4),
                 lhsT_scale=gs[e][:, cols],
                 rhs=ww[:, e, :].bitcast(FP4X4),
-                rhs_scale=ws[:, e, :],
+                rhs_scale=ws[e],
                 start=True,
                 stop=True,
             )
 
         def gelu_side(j):
-            a = psum.tile([P, H], F32, name="a", tag="ring", bufs=5)
-            product(a, j, w1w, w1s)
+            a = psum.tile([P, H], F32, name="a", tag="bank%d" % (j % 4))
+            product(a, j, w1w, [w1s_first[:]] + [w1s[:, e, :] for e in range(E - 1)])
             if j < 7:
                 g = work.tile([P, H], F32, name="g", align_bytes=64)
             else:
@@ -110,11 +113,8 @@ def tile_moe_pkd_glu_gelu_kernel(
             gelus[j] = g
 
         def linear_side(j):
-            if j < 3:
-                b = psum.tile([P, H], F32, name="b", tag="side", bufs=3)
-            else:
-                b = psum.tile([P, H], F32, name="b", tag="ring", bufs=5)
-            product(b, j, w3w, w3s)
+            b = psum.tile([P, H], F32, name="b", tag="bank%d" % (4, 5, 6, 7, 4, 5, 0, 1)[j])
+            product(b, j, w3w, [w3s[:, e, :] for e in range(E)])
             h = work.tile([P, H], BF16, name="h", align_bytes=64)
             nc.vector.tensor_tensor(
                 h[:].rearrange("s (u p d) -> s u p d", u=2, d=2),
@@ -124,9 +124,9 @@ def tile_moe_pkd_glu_gelu_kernel(
             )
             hs[j] = h
 
-        def turn(tiles):
+        def turn(tiles, bank):
             width = P * len(tiles)
-            turned = psum.tile([P, 2, width], F32, name="turned", tag="ring", bufs=5)
+            turned = psum.tile([P, 2, width], F32, name="turned", tag="bank%d" % bank)
             for n, j in enumerate(tiles):
                 words = hs[j][:].bitcast(F32)
                 for u in range(2):
@@ -135,16 +135,13 @@ def tile_moe_pkd_glu_gelu_kernel(
             nc.scalar.copy(hT[:].bitcast(F32).rearrange("p (s u) -> p s u", u=2), turned[:].rearrange("p u s -> p s u"))
             hTs[tiles] = hT
 
-        def second_layer(tiles):
+        def second_layer(tiles, bank):
             width = P * len(tiles)
             e = tiles[0] // 2
             hq = hq_all[:, tiles[0] * P : tiles[0] * P + width]
             hqs = work.tile([P, width], U8, name="hqs", align_bytes=64)
             nc.vector.quantize_mx(out=hq.bitcast(FP8X4), scales=hqs[:], in_=hTs[tiles][:])
-            if len(tiles) == 2:
-                y = psum.tile([P, width], F32, name="y", tag="side", bufs=3)
-            else:
-                y = psum.tile([P, width], F32, name="y", tag="ring", bufs=5)
+            y = psum.tile([P, width], F32, name="y", tag="bank%d" % bank)
             nc.tensor.matmul_mx(
                 out=y[:],
                 lhsT=w2w[:, e, :].bitcast(FP4X4),
@@ -154,33 +151,31 @@ def tile_moe_pkd_glu_gelu_kernel(
                 start=True,
                 stop=True,
             )
-            if len(tiles) == 2:
+            if tiles != (4, 5):
                 nc.scalar.copy(ys[:, tiles[0] * P : tiles[0] * P + width], y[:])
             else:
                 nc.vector.tensor_copy(ys[:, tiles[0] * P : tiles[0] * P + width], y[:])
 
         for e in range(E):
-            gather(e)
+            gather(e, 0, C)
         w2w = keep.tile([P, E, 2 * N], U8, name="w2w", tag="early_scales", align_bytes=64)
         load_words(nc.sync, w2w, w2_words, 0, 4)
         gate_sb = keep.tile([P, 2, T], F32, name="gate_sb", tag="early_words", align_bytes=64)
         nc.sync.dma_start(gate_sb[:], gate.rearrange("g n t -> n g t"))
-        for j in range(8):
+        for j in range(4):
             gelu_side(j)
         for j in range(4):
             linear_side(j)
-        turn((0, 1))
-        linear_side(4)
-        linear_side(5)
-        turn((2, 3))
-        linear_side(6)
-        linear_side(7)
-        turn((4, 5))
-        turn((6,))
-        turn((7,))
+        for j in range(4, 8):
+            gelu_side(j)
+        for j in range(4, 8):
+            linear_side(j)
+        groups = ((0, 1), (2, 3), (4, 5), (6,), (7,))
+        for tiles, bank in zip(groups, (6, 7, 2, 3, 4)):
+            turn(tiles, bank)
         hq_all = keep.tile([P, E * C], U32, name="hq_all", tag="last", align_bytes=64)
-        for tiles in ((0, 1), (2, 3), (4, 5), (6,), (7,)):
-            second_layer(tiles)
+        for tiles, bank in zip(groups, (5, 0, 1, 6, 7)):
+            second_layer(tiles, bank)
 
         first = keep.tile([P, T], F32, name="first", align_bytes=64)
         second = keep.tile([P, T], F32, name="second", align_bytes=64)

@@ -36,14 +36,12 @@ def tile_moe_pkd_glu_gelu_kernel(
         xs = keep.tile([P, T], U8, name="xs", tag="early_scales", align_bytes=64)
         w1w = keep.tile([P, E, 2 * H], U8, name="w1w", align_bytes=64)
         w3w = keep.tile([P, E, 2 * H], U8, name="w3w", align_bytes=64)
-        w1s_first = keep.tile([P, H], U8, name="w1s_first", align_bytes=64)
-        w1s = keep.tile([P, E - 1, H], U8, name="w1s", align_bytes=64)
+        w1s = keep.tile([P, E, H], U8, name="w1s", align_bytes=64)
         w3s = keep.tile([P, E, H], U8, name="w3s", align_bytes=64)
         w2s = keep.tile([P, E, N], U8, name="w2s", align_bytes=64)
         ident = keep.tile([P, P], F32, name="ident", align_bytes=64)
         ys = keep.tile([P, E * C], F32, name="ys", align_bytes=64)
 
-        nc.gpsimd.memset(w1s_first[96:, :].bitcast(I32), 0)
         nc.gpsimd.memset(w1s[:].rearrange("p e n -> p (e n)").bitcast(I32), 0)
         nc.vector.memset(ident[:], 0.0)
         make_identity(nc, ident[:], nomemset=True)
@@ -67,9 +65,8 @@ def tile_moe_pkd_glu_gelu_kernel(
             queue.dma_start(xs[32 * q : 32 * q + 32, :].bitcast(I32), rows.unsqueeze(0).to_broadcast([8, 4, T // 4]))
         nc.scalar.dma_start(xw[:].bitcast(I32), x_words[0].rearrange("p t r -> p (t r)").bitcast(I32))
         load_words(nc.sync, w1w, w1_words, 0, 2)
-        wrapped = w1_scales.rearrange("e s r n -> (e s r) n")[0:28, :].bitcast(I32)
-        nc.scalar.dma_start(w1s_first[0:112, :].bitcast(I32), wrapped.unsqueeze(0).to_broadcast([4, 28, H // 4]))
-        load_scales(nc.sync, w1s, w1_scales[1:], range(4))
+        load_scales(nc.scalar, w1s, w1_scales, (0,))
+        load_scales(nc.sync, w1s, w1_scales, (1, 2, 3))
         load_words(nc.sync, w3w, w3_words, 0, 2)
         load_scales(nc.sync, w3s, w3_scales, range(4))
         load_words(nc.sync, w1w, w1_words, 2, 4)
@@ -102,7 +99,7 @@ def tile_moe_pkd_glu_gelu_kernel(
 
         def gelu_side(j):
             a = psum.tile([P, H], F32, name="a", tag="bank%d" % (j % 4))
-            product(a, j, w1w, [w1s_first[:]] + [w1s[:, e, :] for e in range(E - 1)])
+            product(a, j, w1w, [w1s[:, e, :] for e in range(E)])
             if j < 7:
                 g = work.tile([P, H], F32, name="g", align_bytes=64)
             else:

@@ -73,7 +73,6 @@ def tile_moe_pkd_glu_gelu_kernel(
         load_words(nc.sync, w3w, w3_words, 2, 4)
         nc.sync.dma_start(pos1_sb[:], pos1)
         nc.sync.dma_start(pos2_sb[:], pos2)
-        load_scales(nc.sync, w2s, w2_scales, range(4))
 
         gw = [keep.tile([P, C], U32, name="gw%d" % e, align_bytes=64) for e in range(E)]
         gs = [keep.tile([P, C], U8, name="gs%d" % e, align_bytes=64) for e in range(E)]
@@ -82,6 +81,21 @@ def tile_moe_pkd_glu_gelu_kernel(
             picks = offs_sb[:, (e * C + first) // 16 : (e * C + first + count) // 16]
             nc.vector.tensor_copy(gs[e][:, first : first + count], xs[:].indirect(picks))
             nc.vector.tensor_copy(gw[e][:, first : first + count], xw[:].indirect(picks))
+
+        nc.vector.memset(gw[E - 1][:, :P].bitcast(I32), 0)
+        nc.vector.memset(gs[E - 1][:, :P].bitcast(I32), 0)
+        idle = psum.tile([P, H], F32, name="idle", tag="bank7")
+        for rep in range(3):
+            nc.tensor.matmul_mx(
+                out=idle[:],
+                lhsT=gw[E - 1][:, :P].bitcast(FP8X4),
+                lhsT_scale=gs[E - 1][:, :P],
+                rhs=w1w[:, 0, :].bitcast(FP4X4),
+                rhs_scale=w2s[:].rearrange("p e n -> p (e n)"),
+                start=True,
+                stop=True,
+            )
+        load_scales(nc.sync, w2s, w2_scales, range(4))
 
         gelus, hs, hTs = {}, {}, {}
 

@@ -39,13 +39,15 @@ def tile_moe_pkd_glu_gelu_kernel(
         w1s = keep.tile([P, E, H], U8, name="w1s", align_bytes=64)
         w3s = keep.tile([P, E, H], U8, name="w3s", align_bytes=64)
         w2s = keep.tile([P, E, N], U8, name="w2s", align_bytes=64)
+        w2w = keep.tile([P, E, 2 * N], U8, name="w2w", align_bytes=64)
         ident = keep.tile([P, P], F32, name="ident", align_bytes=64)
         ys = keep.tile([P, E * C], F32, name="ys", align_bytes=64)
 
-        nc.gpsimd.memset(w1s[:].rearrange("p e n -> p (e n)").bitcast(I32), 0)
+        for plane in (w1s, w3s):
+            nc.vector.memset(plane[:].rearrange("p e n -> p (e n)").bitcast(I32), 0)
         nc.vector.memset(ident[:], 0.0)
         make_identity(nc, ident[:], nomemset=True)
-        for plane in (w3s, w2s):
+        for plane in (w2s, w2w):
             nc.vector.memset(plane[:].rearrange("p e n -> p (e n)").bitcast(I32), 0)
 
         def load_words(queue, dst, src, e0, e1):
@@ -90,12 +92,13 @@ def tile_moe_pkd_glu_gelu_kernel(
                 out=idle[:],
                 lhsT=gw[E - 1][:, :P].bitcast(FP8X4),
                 lhsT_scale=gs[E - 1][:, :P],
-                rhs=w1w[:, 0, :].bitcast(FP4X4),
+                rhs=w2w[:].rearrange("p e n -> p (e n)").bitcast(FP4X4),
                 rhs_scale=w2s[:].rearrange("p e n -> p (e n)"),
                 start=True,
                 stop=True,
             )
         load_scales(nc.sync, w2s, w2_scales, range(4))
+        load_words(nc.sync, w2w, w2_words, 0, 4)
 
         gelus, hs, hTs = {}, {}, {}
 
@@ -126,13 +129,23 @@ def tile_moe_pkd_glu_gelu_kernel(
         def linear_side(j):
             b = psum.tile([P, H], F32, name="b", tag="bank%d" % (4, 5, 6, 7, 4, 5, 0, 1)[j])
             product(b, j, w3w, [w3s[:, e, :] for e in range(E)])
-            h = work.tile([P, H], BF16, name="h", align_bytes=64)
-            nc.vector.tensor_tensor(
-                h[:].rearrange("s (u p d) -> s u p d", u=2, d=2),
-                b[:].rearrange("s (p u d) -> s u p d", u=2, d=2),
-                gelus[j][:].rearrange("s (u p d) -> s u p d", u=2, d=2),
-                MULT,
-            )
+            if j == 0:
+                h = keep.tile([P, H], BF16, name="h_held", tag="early_words", align_bytes=64)
+            else:
+                h = work.tile([P, H], BF16, name="h", align_bytes=64)
+            if j in (0,):
+                lin = work.tile([P, H], F32, name="lin", align_bytes=64)
+                nc.scalar.copy(
+                    lin[:].rearrange("s (u p d) -> s u p d", u=2, d=2), b[:].rearrange("s (p u d) -> s u p d", u=2, d=2)
+                )
+                nc.gpsimd.tensor_tensor(h[:], lin[:], gelus[j][:], MULT)
+            else:
+                nc.vector.tensor_tensor(
+                    h[:].rearrange("s (u p d) -> s u p d", u=2, d=2),
+                    b[:].rearrange("s (p u d) -> s u p d", u=2, d=2),
+                    gelus[j][:].rearrange("s (u p d) -> s u p d", u=2, d=2),
+                    MULT,
+                )
             hs[j] = h
 
         def turn(tiles, bank):
@@ -169,9 +182,7 @@ def tile_moe_pkd_glu_gelu_kernel(
 
         for e in range(E):
             gather(e, 0, C)
-        w2w = keep.tile([P, E, 2 * N], U8, name="w2w", tag="early_scales", align_bytes=64)
-        load_words(nc.sync, w2w, w2_words, 0, 4)
-        gate_sb = keep.tile([P, 2, T], F32, name="gate_sb", tag="early_words", align_bytes=64)
+        gate_sb = keep.tile([P, 2, T], F32, name="gate_sb", tag="early_scales", align_bytes=64)
         nc.sync.dma_start(gate_sb[:], gate.rearrange("g n t -> n g t"))
         for j in range(4):
             gelu_side(j)

@@ -66,9 +66,8 @@ def tile_moe_pkd_glu_gelu_kernel(
             queue = nc.sync if q < 2 else nc.scalar
             queue.dma_start(xs[32 * q : 32 * q + 32, :].bitcast(I32), rows.unsqueeze(0).to_broadcast([8, 4, T // 4]))
         nc.scalar.dma_start(xw[:].bitcast(I32), x_words[0].rearrange("p t r -> p (t r)").bitcast(I32))
-        load_words(nc.sync, w1w, w1_words, 0, 2)
-        load_scales(nc.scalar, w1s, w1_scales, (0,))
-        load_scales(nc.sync, w1s, w1_scales, (1, 2, 3))
+        load_words(nc.scalar, w1w, w1_words, 0, 2)
+        load_scales(nc.sync, w1s, w1_scales, range(4))
         load_words(nc.sync, w3w, w3_words, 0, 2)
         load_scales(nc.sync, w3s, w3_scales, range(4))
         load_words(nc.sync, w1w, w1_words, 2, 4)

@@ -53,11 +53,11 @@ def tile_moe_pkd_glu_gelu_kernel(
         def load_words(queue, dst, src, e0, e1):
             queue.dma_start(dst[:, e0:e1, :].bitcast(I32), src[e0:e1, 0].rearrange("e p n -> p e n").bitcast(I32))
 
-        def load_scales(queue, dst, src, quadrants):
-            for q in quadrants:
-                queue.dma_start(
-                    dst[32 * q : 32 * q + 4, :, :].bitcast(I32),
-                    src[:, 0, 4 * q : 4 * q + 4, :].rearrange("e r n -> r e n").bitcast(I32),
+        def load_scales(dst, src, e0, e1):
+            for r in range(4):
+                nc.sync.dma_start(
+                    dst[r:P:32, e0:e1, :].bitcast(I32),
+                    src[e0:e1, 0, r:16:4, :].rearrange("e q n -> q e n").bitcast(I32),
                 )
 
         nc.sync.dma_start(offs_sb[:], offs)
@@ -67,9 +67,9 @@ def tile_moe_pkd_glu_gelu_kernel(
             queue.dma_start(xs[32 * q : 32 * q + 32, :].bitcast(I32), rows.unsqueeze(0).to_broadcast([8, 4, T // 4]))
         nc.scalar.dma_start(xw[:].bitcast(I32), x_words[0].rearrange("p t r -> p (t r)").bitcast(I32))
         load_words(nc.scalar, w1w, w1_words, 0, 2)
-        load_scales(nc.sync, w1s, w1_scales, range(4))
+        load_scales(w1s, w1_scales, 0, E)
+        load_scales(w3s, w3_scales, 0, E)
         load_words(nc.sync, w3w, w3_words, 0, 2)
-        load_scales(nc.sync, w3s, w3_scales, range(4))
         load_words(nc.sync, w1w, w1_words, 2, 4)
         load_words(nc.sync, w3w, w3_words, 2, 4)
         nc.sync.dma_start(pos1_sb[:], pos1)
@@ -96,7 +96,7 @@ def tile_moe_pkd_glu_gelu_kernel(
                 start=True,
                 stop=True,
             )
-        load_scales(nc.sync, w2s, w2_scales, range(4))
+        load_scales(w2s, w2_scales, 0, E)
         load_words(nc.sync, w2w, w2_words, 0, 4)
 
         gelus, hs, hTs = {}, {}, {}

@@ -36,14 +36,17 @@ def tile_moe_pkd_glu_gelu_kernel(
         xs = keep.tile([P, T], U8, name="xs", tag="early_scales", align_bytes=64)
         w1w = keep.tile([P, E, 2 * H], U8, name="w1w", align_bytes=64)
         w3w = keep.tile([P, E, 2 * H], U8, name="w3w", align_bytes=64)
-        w1s = keep.tile([P, E, H], U8, name="w1s", align_bytes=64)
+        w1s_first = [keep.tile([P, H], U8, name="w1s_first%d" % e, align_bytes=64) for e in range(2)]
+        w1s = keep.tile([P, E - 2, H], U8, name="w1s", align_bytes=64)
         w3s = keep.tile([P, E, H], U8, name="w3s", align_bytes=64)
         w2s = keep.tile([P, E, N], U8, name="w2s", align_bytes=64)
         w2w = keep.tile([P, E, 2 * N], U8, name="w2w", align_bytes=64)
         ident = keep.tile([P, P], F32, name="ident", align_bytes=64)
         ys = keep.tile([P, E * C], F32, name="ys", align_bytes=64)
 
-        for plane in (w1s, w3s):
+        for plane in w1s_first:
+            nc.vector.memset(plane[:].bitcast(I32), 0)
+        for plane in (w3s, w1s):
             nc.vector.memset(plane[:].rearrange("p e n -> p (e n)").bitcast(I32), 0)
         nc.vector.memset(ident[:], 0.0)
         make_identity(nc, ident[:], nomemset=True)
@@ -56,7 +59,7 @@ def tile_moe_pkd_glu_gelu_kernel(
         def load_scales(dst, src, e0, e1):
             for r in range(4):
                 nc.sync.dma_start(
-                    dst[r:P:32, e0:e1, :].bitcast(I32),
+                    dst[r:P:32, :, :].bitcast(I32),
                     src[e0:e1, 0, r:16:4, :].rearrange("e q n -> q e n").bitcast(I32),
                 )
 
@@ -67,10 +70,13 @@ def tile_moe_pkd_glu_gelu_kernel(
             queue.dma_start(xs[32 * q : 32 * q + 32, :].bitcast(I32), rows.unsqueeze(0).to_broadcast([8, 4, T // 4]))
         nc.scalar.dma_start(xw[:].bitcast(I32), x_words[0].rearrange("p t r -> p (t r)").bitcast(I32))
         load_words(nc.scalar, w1w, w1_words, 0, 2)
-        load_scales(w1s, w1_scales, 0, E)
+        for e in range(2):
+            wrapped = w1_scales.rearrange("e s q n -> (e s q) n")[16 * e : 16 * e + 28, :].bitcast(I32)
+            nc.sync.dma_start(w1s_first[e][0:112, :].bitcast(I32), wrapped.unsqueeze(0).to_broadcast([4, 28, H // 4]))
         load_scales(w3s, w3_scales, 0, E)
         load_words(nc.sync, w3w, w3_words, 0, 2)
         load_words(nc.sync, w1w, w1_words, 2, 4)
+        load_scales(w1s, w1_scales, 2, E)
         load_words(nc.sync, w3w, w3_words, 2, 4)
         nc.sync.dma_start(pos1_sb[:], pos1)
         nc.sync.dma_start(pos2_sb[:], pos2)
@@ -115,7 +121,7 @@ def tile_moe_pkd_glu_gelu_kernel(
 
         def gelu_side(j):
             a = psum.tile([P, H], F32, name="a", tag="bank%d" % (j % 4))
-            product(a, j, w1w, [w1s[:, e, :] for e in range(E)])
+            product(a, j, w1w, [t[:] for t in w1s_first] + [w1s[:, e, :] for e in range(E - 2)])
             if j < 7:
                 g = work.tile([P, H], F32, name="g", align_bytes=64)
             else:
@@ -126,18 +132,34 @@ def tile_moe_pkd_glu_gelu_kernel(
             gelus[j] = g
 
         def linear_side(j):
-            b = psum.tile([P, H], F32, name="b", tag="bank%d" % (4, 5, 6, 7, 4, 5, 0, 1)[j])
+            b = psum.tile([P, H], F32, name="b", tag="bank%d" % (4, 5, 6, 7, 4, 5, 6, 7)[j])
             product(b, j, w3w, [w3s[:, e, :] for e in range(E)])
             if j == 0:
                 h = keep.tile([P, H], BF16, name="h_held", tag="early_words", align_bytes=64)
             else:
                 h = work.tile([P, H], BF16, name="h", align_bytes=64)
-            if j in (0,):
+            if j == 0:
                 lin = work.tile([P, H], F32, name="lin", align_bytes=64)
                 nc.scalar.copy(
                     lin[:].rearrange("s (u p d) -> s u p d", u=2, d=2), b[:].rearrange("s (p u d) -> s u p d", u=2, d=2)
                 )
                 nc.gpsimd.tensor_tensor(h[:], lin[:], gelus[j][:], MULT)
+            elif j == 3:
+                half = H // 2
+                lin = work.tile([P, half], F32, name="lin_half", align_bytes=64)
+                nc.scalar.copy(
+                    lin[:].rearrange("s (u p d) -> s u p d", u=2, d=2),
+                    b[:, :half].rearrange("s (p u d) -> s u p d", u=2, d=2),
+                )
+                h_u = h[:].rearrange("s (u q) -> s u q", u=2)
+                g_u = gelus[j][:].rearrange("s (u q) -> s u q", u=2)
+                nc.gpsimd.tensor_tensor(h_u[:, :, :P], lin[:].rearrange("s (u q) -> s u q", u=2), g_u[:, :, :P], MULT)
+                nc.vector.tensor_tensor(
+                    h_u[:, :, P:].rearrange("s u (p d) -> s u p d", d=2),
+                    b[:, half:].rearrange("s (p u d) -> s u p d", u=2, d=2),
+                    g_u[:, :, P:].rearrange("s u (p d) -> s u p d", d=2),
+                    MULT,
+                )
             else:
                 nc.vector.tensor_tensor(
                     h[:].rearrange("s (u p d) -> s u p d", u=2, d=2),
@@ -192,10 +214,10 @@ def tile_moe_pkd_glu_gelu_kernel(
         for j in range(4, 8):
             linear_side(j)
         groups = ((0, 1), (2, 3), (4, 5), (6,), (7,))
-        for tiles, bank in zip(groups, (6, 7, 2, 3, 4)):
+        for tiles, bank in zip(groups, (1, 2, 0, 3, 4)):
             turn(tiles, bank)
-        hq_all = keep.tile([P, E * C], U32, name="hq_all", tag="last", align_bytes=64)
-        for tiles, bank in zip(groups, (5, 0, 1, 6, 7)):
+        hq_all = keep.tile([P, E * C], U32, name="hq_all", align_bytes=64)
+        for tiles, bank in zip(groups, (5, 6, 1, 7, 2)):
             second_layer(tiles, bank)
 
         first = keep.tile([P, T], F32, name="first", align_bytes=64)

@@ -5,6 +5,7 @@ from concourse.masks import make_identity
 
 K, T, E, C, H, N = 512, 512, 4, 256, 512, 128
 P = 128
+TAIL = 192
 FLOPS = 2 * E * C * (2 * K * H + H * N)
 
 F32 = mybir.dt.float32
@@ -33,11 +34,11 @@ def tile_moe_pkd_glu_gelu_kernel(
         pos1_sb = keep.tile([P, T // 16], U16, name="pos1_sb")
         pos2_sb = keep.tile([P, T // 16], U16, name="pos2_sb")
         xw = keep.tile([P, T], U32, name="xw", tag="early_words", align_bytes=64)
-        xs = keep.tile([P, T], U8, name="xs", tag="early_scales", align_bytes=64)
+        xs = keep.tile([P, T + TAIL], U8, name="xs", tag="early_scales", align_bytes=64)
         w1w = keep.tile([P, E, 2 * H], U8, name="w1w", align_bytes=64)
         w3w = keep.tile([P, E, 2 * H], U8, name="w3w", align_bytes=64)
-        w1s_first = [keep.tile([P, H], U8, name="w1s_first%d" % e, align_bytes=64) for e in range(2)]
-        w1s = keep.tile([P, E - 2, H], U8, name="w1s", align_bytes=64)
+        w1s_first = [keep.tile([P, H], U8, name="w1s_first%d" % e, align_bytes=64) for e in range(1)]
+        w1s = keep.tile([P, E - 1, H], U8, name="w1s", align_bytes=64)
         w3s = keep.tile([P, E, H], U8, name="w3s", align_bytes=64)
         w2s = keep.tile([P, E, N], U8, name="w2s", align_bytes=64)
         w2w = keep.tile([P, E, 2 * N], U8, name="w2w", align_bytes=64)
@@ -46,7 +47,7 @@ def tile_moe_pkd_glu_gelu_kernel(
 
         for plane in w1s_first:
             nc.vector.memset(plane[:].bitcast(I32), 0)
-        for plane in (w3s, w1s):
+        for plane in (w1s, w3s):
             nc.vector.memset(plane[:].rearrange("p e n -> p (e n)").bitcast(I32), 0)
         nc.vector.memset(ident[:], 0.0)
         make_identity(nc, ident[:], nomemset=True)
@@ -67,28 +68,34 @@ def tile_moe_pkd_glu_gelu_kernel(
         for q in range(4):
             rows = x_scales[0, 4 * q : 4 * q + 4, :].bitcast(I32)
             queue = nc.sync if q < 2 else nc.scalar
-            queue.dma_start(xs[32 * q : 32 * q + 32, :].bitcast(I32), rows.unsqueeze(0).to_broadcast([8, 4, T // 4]))
+            queue.dma_start(xs[32 * q : 32 * q + 32, :T].bitcast(I32), rows.unsqueeze(0).to_broadcast([8, 4, T // 4]))
         nc.scalar.dma_start(xw[:].bitcast(I32), x_words[0].rearrange("p t r -> p (t r)").bitcast(I32))
         load_words(nc.scalar, w1w, w1_words, 0, 2)
-        for e in range(2):
+        for e in range(1):
             wrapped = w1_scales.rearrange("e s q n -> (e s q) n")[16 * e : 16 * e + 28, :].bitcast(I32)
             nc.sync.dma_start(w1s_first[e][0:112, :].bitcast(I32), wrapped.unsqueeze(0).to_broadcast([4, 28, H // 4]))
-        load_scales(w3s, w3_scales, 0, E)
+        load_scales(w1s, w1_scales, 1, E)
         load_words(nc.sync, w3w, w3_words, 0, 2)
+        load_scales(w3s, w3_scales, 0, E)
         load_words(nc.sync, w1w, w1_words, 2, 4)
-        load_scales(w1s, w1_scales, 2, E)
         load_words(nc.sync, w3w, w3_words, 2, 4)
         nc.sync.dma_start(pos1_sb[:], pos1)
         nc.sync.dma_start(pos2_sb[:], pos2)
 
         gw = [keep.tile([P, C], U32, name="gw%d" % e, align_bytes=64) for e in range(E)]
-        gs = [keep.tile([P, C], U8, name="gs%d" % e, align_bytes=64) for e in range(E)]
+        gs_late = keep.tile([P, 2 * C], U8, name="gs_late", align_bytes=64)
+        gs = [keep.tile([P, C], U8, name="gs%d" % e, align_bytes=64) for e in range(2)]
+        gs = gs + [gs_late[:, :C], gs_late[:, C:]]
 
         def gather(e, first, count):
             picks = offs_sb[:, (e * C + first) // 16 : (e * C + first + count) // 16]
-            nc.vector.tensor_copy(gs[e][:, first : first + count], xs[:].indirect(picks))
+            if e < 2:
+                nc.vector.tensor_copy(gs[e][:, first : first + count], xs[:].indirect(picks))
+            elif e == 2:
+                nc.vector.tensor_copy(gs_late[:], xs[:].indirect(offs_sb[:, 2 * C // 16 :]))
             nc.vector.tensor_copy(gw[e][:, first : first + count], xw[:].indirect(picks))
 
+        nc.vector.memset(xs[:, T:].bitcast(I32), 0)
         nc.vector.memset(gw[E - 1][:, :P].bitcast(I32), 0)
         nc.vector.memset(gs[E - 1][:, :P].bitcast(I32), 0)
         idle = psum.tile([P, H], F32, name="idle", tag="bank7")
@@ -121,7 +128,7 @@ def tile_moe_pkd_glu_gelu_kernel(
 
         def gelu_side(j):
             a = psum.tile([P, H], F32, name="a", tag="bank%d" % (j % 4))
-            product(a, j, w1w, [t[:] for t in w1s_first] + [w1s[:, e, :] for e in range(E - 2)])
+            product(a, j, w1w, [t[:] for t in w1s_first] + [w1s[:, e, :] for e in range(E - 1)])
             if j < 7:
                 g = work.tile([P, H], F32, name="g", align_bytes=64)
             else:

@@ -64,16 +64,16 @@ def tile_moe_pkd_glu_gelu_kernel(
                     src[e0:e1, 0, r:16:4, :].rearrange("e q n -> q e n").bitcast(I32),
                 )
 
-        nc.sync.dma_start(offs_sb[:], offs)
         for q in range(4):
             rows = x_scales[0, 4 * q : 4 * q + 4, :].bitcast(I32)
-            queue = nc.sync if q < 2 else nc.scalar
+            queue = nc.sync if q < 3 else nc.scalar
             queue.dma_start(xs[32 * q : 32 * q + 32, :T].bitcast(I32), rows.unsqueeze(0).to_broadcast([8, 4, T // 4]))
+        nc.sync.dma_start(offs_sb[:], offs)
         nc.scalar.dma_start(xw[:].bitcast(I32), x_words[0].rearrange("p t r -> p (t r)").bitcast(I32))
-        load_words(nc.scalar, w1w, w1_words, 0, 2)
         for e in range(1):
             wrapped = w1_scales.rearrange("e s q n -> (e s q) n")[16 * e : 16 * e + 28, :].bitcast(I32)
-            nc.sync.dma_start(w1s_first[e][0:112, :].bitcast(I32), wrapped.unsqueeze(0).to_broadcast([4, 28, H // 4]))
+            nc.scalar.dma_start(w1s_first[e][0:112, :].bitcast(I32), wrapped.unsqueeze(0).to_broadcast([4, 28, H // 4]))
+        load_words(nc.scalar, w1w, w1_words, 0, 2)
         load_scales(w1s, w1_scales, 1, E)
         load_words(nc.sync, w3w, w3_words, 0, 2)
         load_scales(w3s, w3_scales, 0, E)

@@ -19,6 +19,7 @@ FP4X4 = mybir.dt.float4_e2m1fn_x4
 MULT = mybir.AluOpType.mult
 ADD = mybir.AluOpType.add
 GELU = mybir.ActivationFunctionType.Gelu_apprx_tanh
+COPY = mybir.ActivationFunctionType.Copy
 
 
 def tile_moe_pkd_glu_gelu_kernel(
@@ -51,8 +52,7 @@ def tile_moe_pkd_glu_gelu_kernel(
             nc.vector.memset(plane[:].rearrange("p e n -> p (e n)").bitcast(I32), 0)
         nc.vector.memset(ident[:], 0.0)
         make_identity(nc, ident[:], nomemset=True)
-        for plane in (w2s, w2w):
-            nc.vector.memset(plane[:].rearrange("p e n -> p (e n)").bitcast(I32), 0)
+        nc.vector.memset(w2s[:].rearrange("p e n -> p (e n)").bitcast(I32), 0)
 
         def load_words(queue, dst, src, e0, e1):
             queue.dma_start(dst[:, e0:e1, :].bitcast(I32), src[e0:e1, 0].rearrange("e p n -> p e n").bitcast(I32))
@@ -96,19 +96,6 @@ def tile_moe_pkd_glu_gelu_kernel(
             nc.vector.tensor_copy(gw[e][:, first : first + count], xw[:].indirect(picks))
 
         nc.vector.memset(xs[:, T:].bitcast(I32), 0)
-        nc.vector.memset(gw[E - 1][:, :P].bitcast(I32), 0)
-        nc.vector.memset(gs[E - 1][:, :P].bitcast(I32), 0)
-        idle = psum.tile([P, H], F32, name="idle", tag="bank7")
-        for rep in range(3):
-            nc.tensor.matmul_mx(
-                out=idle[:],
-                lhsT=gw[E - 1][:, :P].bitcast(FP8X4),
-                lhsT_scale=gs[E - 1][:, :P],
-                rhs=w2w[:].rearrange("p e n -> p (e n)").bitcast(FP4X4),
-                rhs_scale=w2s[:].rearrange("p e n -> p (e n)"),
-                start=True,
-                stop=True,
-            )
         load_scales(w2s, w2_scales, 0, E)
         load_words(nc.sync, w2w, w2_words, 0, 4)
 
@@ -232,9 +219,12 @@ def tile_moe_pkd_glu_gelu_kernel(
         res = keep.tile([P, T], F32, name="res", align_bytes=64)
         halves = (slice(0, T // 2), slice(T // 2, T))
         nc.vector.tensor_tensor(first[:], ys[:].indirect(pos1_sb[:]), gate_sb[:, 0, :], MULT)
+        picked = keep.tile([P, T], F32, name="picked", align_bytes=64)
         for half in halves:
             picks = pos2_sb[:, half.start // 16 : half.stop // 16]
-            nc.vector.tensor_tensor(second[:, half], ys[:].indirect(picks), gate_sb[:, 1, half], MULT)
+            nc.scalar.activation(picked[:, half], ys[:].indirect(picks), COPY)
+        for half in halves:
+            nc.vector.tensor_tensor(second[:, half], picked[:, half], gate_sb[:, 1, half], MULT)
         for half in halves:
             nc.vector.tensor_tensor(res[:, half], first[:, half], second[:, half], ADD)
             nc.sync.dma_start(out[:, half], res[:, half])

@@ -55,7 +55,7 @@ def tile_moe_pkd_glu_gelu_kernel(
         nc.vector.memset(w2s[:].rearrange("p e n -> p (e n)").bitcast(I32), 0)
 
         def load_words(queue, dst, src, e0, e1):
-            queue.dma_start(dst[:, e0:e1, :].bitcast(I32), src[e0:e1, 0].rearrange("e p n -> p e n").bitcast(I32))
+            queue.dma_start(dst[:, e0:e1, :].bitcast(I32), src[e0:e1, 0].bitcast(I32).rearrange("e p n -> p e n"))
 
         def load_scales(dst, src, e0, e1):
             for r in range(4):
@@ -70,10 +70,11 @@ def tile_moe_pkd_glu_gelu_kernel(
             queue.dma_start(xs[32 * q : 32 * q + 32, :T].bitcast(I32), rows.unsqueeze(0).to_broadcast([8, 4, T // 4]))
         nc.sync.dma_start(offs_sb[:], offs)
         nc.scalar.dma_start(xw[:].bitcast(I32), x_words[0].rearrange("p t r -> p (t r)").bitcast(I32))
+        load_words(nc.scalar, w1w, w1_words, 0, 1)
         for e in range(1):
             wrapped = w1_scales.rearrange("e s q n -> (e s q) n")[16 * e : 16 * e + 28, :].bitcast(I32)
             nc.scalar.dma_start(w1s_first[e][0:112, :].bitcast(I32), wrapped.unsqueeze(0).to_broadcast([4, 28, H // 4]))
-        load_words(nc.scalar, w1w, w1_words, 0, 2)
+        load_words(nc.sync, w1w, w1_words, 1, 2)
         load_scales(w1s, w1_scales, 1, E)
         load_words(nc.sync, w3w, w3_words, 0, 2)
         load_scales(w3s, w3_scales, 0, E)
@@ -190,10 +191,7 @@ def tile_moe_pkd_glu_gelu_kernel(
                 start=True,
                 stop=True,
             )
-            if tiles != (4, 5):
-                nc.scalar.copy(ys[:, tiles[0] * P : tiles[0] * P + width], y[:])
-            else:
-                nc.vector.tensor_copy(ys[:, tiles[0] * P : tiles[0] * P + width], y[:])
+            nc.scalar.copy(ys[:, tiles[0] * P : tiles[0] * P + width], y[:])
 
         for e in range(E):
             gather(e, 0, C)

@@ -64,16 +64,17 @@ def tile_moe_pkd_glu_gelu_kernel(
                     src[e0:e1, 0, r:16:4, :].rearrange("e q n -> q e n").bitcast(I32),
                 )
 
+        staged = keep.tile([4, 4, H], U8, name="staged", align_bytes=64)
+        nc.sync.dma_start(staged[:].bitcast(I32), w1_scales[0, 0].bitcast(I32).rearrange("(q r) n -> r q n", r=4))
         for q in range(4):
             rows = x_scales[0, 4 * q : 4 * q + 4, :].bitcast(I32)
-            queue = nc.sync if q < 3 else nc.scalar
+            queue = nc.sync if q < 2 else nc.scalar
             queue.dma_start(xs[32 * q : 32 * q + 32, :T].bitcast(I32), rows.unsqueeze(0).to_broadcast([8, 4, T // 4]))
         nc.sync.dma_start(offs_sb[:], offs)
         nc.scalar.dma_start(xw[:].bitcast(I32), x_words[0].rearrange("p t r -> p (t r)").bitcast(I32))
         load_words(nc.scalar, w1w, w1_words, 0, 1)
-        for e in range(1):
-            wrapped = w1_scales.rearrange("e s q n -> (e s q) n")[16 * e : 16 * e + 28, :].bitcast(I32)
-            nc.scalar.dma_start(w1s_first[e][0:112, :].bitcast(I32), wrapped.unsqueeze(0).to_broadcast([4, 28, H // 4]))
+        for q in range(4):
+            nc.vector.tensor_copy(w1s_first[0][32 * q : 32 * q + 4, :].bitcast(I32), staged[:, q, :].bitcast(I32))
         load_words(nc.sync, w1w, w1_words, 1, 2)
         load_scales(w1s, w1_scales, 1, E)
         load_words(nc.sync, w3w, w3_words, 0, 2)
@@ -94,7 +95,10 @@ def tile_moe_pkd_glu_gelu_kernel(
                 nc.vector.tensor_copy(gs[e][:, first : first + count], xs[:].indirect(picks))
             elif e == 2:
                 nc.vector.tensor_copy(gs_late[:], xs[:].indirect(offs_sb[:, 2 * C // 16 :]))
-            nc.vector.tensor_copy(gw[e][:, first : first + count], xw[:].indirect(picks))
+            step = P if e < 2 else C
+            for lo in range(0, C, step):
+                picks = offs_sb[:, (e * C + lo) // 16 : (e * C + lo + step) // 16]
+                nc.vector.tensor_copy(gw[e][:, lo : lo + step], xw[:].indirect(picks))
 
         nc.vector.memset(xs[:, T:].bitcast(I32), 0)
         load_scales(w2s, w2_scales, 0, E)

@@ -40,7 +40,8 @@ def tile_moe_pkd_glu_gelu_kernel(
         w3w = keep.tile([P, E, 2 * H], U8, name="w3w", align_bytes=64)
         w1s_first = [keep.tile([P, H], U8, name="w1s_first%d" % e, align_bytes=64) for e in range(1)]
         w1s = keep.tile([P, E - 1, H], U8, name="w1s", align_bytes=64)
-        w3s = keep.tile([P, E, H], U8, name="w3s", align_bytes=64)
+        w3s_first = keep.tile([P, H], U8, name="w3s_first", align_bytes=64)
+        w3s = keep.tile([P, E - 1, H], U8, name="w3s", align_bytes=64)
         w2s = keep.tile([P, E, N], U8, name="w2s", align_bytes=64)
         w2w = keep.tile([P, E, 2 * N], U8, name="w2w", align_bytes=64)
         ident = keep.tile([P, P], F32, name="ident", align_bytes=64)
@@ -48,6 +49,7 @@ def tile_moe_pkd_glu_gelu_kernel(
 
         for plane in w1s_first:
             nc.vector.memset(plane[:].bitcast(I32), 0)
+        nc.vector.memset(w3s_first[:].bitcast(I32), 0)
         for plane in (w1s, w3s):
             nc.vector.memset(plane[:].rearrange("p e n -> p (e n)").bitcast(I32), 0)
         nc.vector.memset(ident[:], 0.0)
@@ -75,10 +77,13 @@ def tile_moe_pkd_glu_gelu_kernel(
         load_words(nc.scalar, w1w, w1_words, 0, 1)
         for q in range(4):
             nc.vector.tensor_copy(w1s_first[0][32 * q : 32 * q + 4, :].bitcast(I32), staged[:, q, :].bitcast(I32))
+        load_words(nc.sync, w3w, w3_words, 0, 1)
+        wrapped = w3_scales.rearrange("e s q n -> (e s q) n")[0:28, :].bitcast(I32)
+        nc.sync.dma_start(w3s_first[0:112, :].bitcast(I32), wrapped.unsqueeze(0).to_broadcast([4, 28, H // 4]))
         load_words(nc.sync, w1w, w1_words, 1, 2)
         load_scales(w1s, w1_scales, 1, E)
-        load_words(nc.sync, w3w, w3_words, 0, 2)
-        load_scales(w3s, w3_scales, 0, E)
+        load_words(nc.sync, w3w, w3_words, 1, 2)
+        load_scales(w3s, w3_scales, 1, E)
         load_words(nc.sync, w1w, w1_words, 2, 4)
         load_words(nc.sync, w3w, w3_words, 2, 4)
         nc.sync.dma_start(pos1_sb[:], pos1)
@@ -95,7 +100,7 @@ def tile_moe_pkd_glu_gelu_kernel(
                 nc.vector.tensor_copy(gs[e][:, first : first + count], xs[:].indirect(picks))
             elif e == 2:
                 nc.vector.tensor_copy(gs_late[:], xs[:].indirect(offs_sb[:, 2 * C // 16 :]))
-            step = P if e < 2 else C
+            step = P if e == 0 else C
             for lo in range(0, C, step):
                 picks = offs_sb[:, (e * C + lo) // 16 : (e * C + lo + step) // 16]
                 nc.vector.tensor_copy(gw[e][:, lo : lo + step], xw[:].indirect(picks))
@@ -119,7 +124,7 @@ def tile_moe_pkd_glu_gelu_kernel(
             )
 
         def gelu_side(j):
-            a = psum.tile([P, H], F32, name="a", tag="bank%d" % (j % 4))
+            a = psum.tile([P, H], F32, name="a", tag="bank%d" % (0, 1, 2, 3, 0, 1, 4, 5)[j])
             product(a, j, w1w, [t[:] for t in w1s_first] + [w1s[:, e, :] for e in range(E - 1)])
             if j < 7:
                 g = work.tile([P, H], F32, name="g", align_bytes=64)
@@ -131,34 +136,15 @@ def tile_moe_pkd_glu_gelu_kernel(
             gelus[j] = g
 
         def linear_side(j):
-            b = psum.tile([P, H], F32, name="b", tag="bank%d" % (4, 5, 6, 7, 4, 5, 6, 7)[j])
-            product(b, j, w3w, [w3s[:, e, :] for e in range(E)])
-            if j == 0:
-                h = keep.tile([P, H], BF16, name="h_held", tag="early_words", align_bytes=64)
-            else:
-                h = work.tile([P, H], BF16, name="h", align_bytes=64)
-            if j == 0:
+            b = psum.tile([P, H], F32, name="b", tag="bank%d" % (4, 5, 6, 7, 2, 3, 6, 7)[j])
+            product(b, j, w3w, [w3s_first[:]] + [w3s[:, e, :] for e in range(E - 1)])
+            h = work.tile([P, H], BF16, name="h", align_bytes=64)
+            if j < 2:
                 lin = work.tile([P, H], F32, name="lin", align_bytes=64)
                 nc.scalar.copy(
                     lin[:].rearrange("s (u p d) -> s u p d", u=2, d=2), b[:].rearrange("s (p u d) -> s u p d", u=2, d=2)
                 )
                 nc.gpsimd.tensor_tensor(h[:], lin[:], gelus[j][:], MULT)
-            elif j == 3:
-                half = H // 2
-                lin = work.tile([P, half], F32, name="lin_half", align_bytes=64)
-                nc.scalar.copy(
-                    lin[:].rearrange("s (u p d) -> s u p d", u=2, d=2),
-                    b[:, :half].rearrange("s (p u d) -> s u p d", u=2, d=2),
-                )
-                h_u = h[:].rearrange("s (u q) -> s u q", u=2)
-                g_u = gelus[j][:].rearrange("s (u q) -> s u q", u=2)
-                nc.gpsimd.tensor_tensor(h_u[:, :, :P], lin[:].rearrange("s (u q) -> s u q", u=2), g_u[:, :, :P], MULT)
-                nc.vector.tensor_tensor(
-                    h_u[:, :, P:].rearrange("s u (p d) -> s u p d", d=2),
-                    b[:, half:].rearrange("s (p u d) -> s u p d", u=2, d=2),
-                    g_u[:, :, P:].rearrange("s u (p d) -> s u p d", d=2),
-                    MULT,
-                )
             else:
                 nc.vector.tensor_tensor(
                     h[:].rearrange("s (u p d) -> s u p d", u=2, d=2),
@@ -201,19 +187,20 @@ def tile_moe_pkd_glu_gelu_kernel(
             gather(e, 0, C)
         gate_sb = keep.tile([P, 2, T], F32, name="gate_sb", tag="early_scales", align_bytes=64)
         nc.sync.dma_start(gate_sb[:], gate.rearrange("g n t -> n g t"))
-        for j in range(4):
-            gelu_side(j)
-        for j in range(4):
-            linear_side(j)
+        for pair in ((0, 1), (2, 3)):
+            for j in pair:
+                gelu_side(j)
+            for j in pair:
+                linear_side(j)
         for j in range(4, 8):
             gelu_side(j)
         for j in range(4, 8):
             linear_side(j)
         groups = ((0, 1), (2, 3), (4, 5), (6,), (7,))
-        for tiles, bank in zip(groups, (1, 2, 0, 3, 4)):
+        for tiles, bank in zip(groups, (1, 4, 0, 5, 2)):
             turn(tiles, bank)
         hq_all = keep.tile([P, E * C], U32, name="hq_all", align_bytes=64)
-        for tiles, bank in zip(groups, (5, 6, 1, 7, 2)):
+        for tiles, bank in zip(groups, (3, 6, 1, 7, 4)):
             second_layer(tiles, bank)
 
         first = keep.tile([P, T], F32, name="first", align_bytes=64)

@@ -66,17 +66,15 @@ def tile_moe_pkd_glu_gelu_kernel(
                     src[e0:e1, 0, r:16:4, :].rearrange("e q n -> q e n").bitcast(I32),
                 )
 
-        staged = keep.tile([4, 4, H], U8, name="staged", align_bytes=64)
-        nc.sync.dma_start(staged[:].bitcast(I32), w1_scales[0, 0].bitcast(I32).rearrange("(q r) n -> r q n", r=4))
         for q in range(4):
             rows = x_scales[0, 4 * q : 4 * q + 4, :].bitcast(I32)
-            queue = nc.sync if q < 2 else nc.scalar
+            queue = nc.sync if q < 3 else nc.scalar
             queue.dma_start(xs[32 * q : 32 * q + 32, :T].bitcast(I32), rows.unsqueeze(0).to_broadcast([8, 4, T // 4]))
         nc.sync.dma_start(offs_sb[:], offs)
         nc.scalar.dma_start(xw[:].bitcast(I32), x_words[0].rearrange("p t r -> p (t r)").bitcast(I32))
         load_words(nc.scalar, w1w, w1_words, 0, 1)
-        for q in range(4):
-            nc.vector.tensor_copy(w1s_first[0][32 * q : 32 * q + 4, :].bitcast(I32), staged[:, q, :].bitcast(I32))
+        wrapped = w1_scales.rearrange("e s q n -> (e s q) n")[0:28, :].bitcast(I32)
+        nc.scalar.dma_start(w1s_first[0][0:112, :].bitcast(I32), wrapped.unsqueeze(0).to_broadcast([4, 28, H // 4]))
         load_words(nc.sync, w3w, w3_words, 0, 1)
         wrapped = w3_scales.rearrange("e s q n -> (e s q) n")[0:28, :].bitcast(I32)
         nc.sync.dma_start(w3s_first[0:112, :].bitcast(I32), wrapped.unsqueeze(0).to_broadcast([4, 28, H // 4]))

@@ -40,8 +40,7 @@ def tile_moe_pkd_glu_gelu_kernel(
         w3w = keep.tile([P, E, 2 * H], U8, name="w3w", align_bytes=64)
         w1s_first = [keep.tile([P, H], U8, name="w1s_first%d" % e, align_bytes=64) for e in range(1)]
         w1s = keep.tile([P, E - 1, H], U8, name="w1s", align_bytes=64)
-        w3s_first = keep.tile([P, H], U8, name="w3s_first", align_bytes=64)
-        w3s = keep.tile([P, E - 1, H], U8, name="w3s", align_bytes=64)
+        w3s = keep.tile([P, E, H], U8, name="w3s", align_bytes=64)
         w2s = keep.tile([P, E, N], U8, name="w2s", align_bytes=64)
         w2w = keep.tile([P, E, 2 * N], U8, name="w2w", align_bytes=64)
         ident = keep.tile([P, P], F32, name="ident", align_bytes=64)
@@ -49,8 +48,7 @@ def tile_moe_pkd_glu_gelu_kernel(
 
         for plane in w1s_first:
             nc.vector.memset(plane[:].bitcast(I32), 0)
-        nc.vector.memset(w3s_first[:].bitcast(I32), 0)
-        for plane in (w1s, w3s):
+        for plane in (w3s, w1s):
             nc.vector.memset(plane[:].rearrange("p e n -> p (e n)").bitcast(I32), 0)
         nc.vector.memset(ident[:], 0.0)
         make_identity(nc, ident[:], nomemset=True)
@@ -76,12 +74,10 @@ def tile_moe_pkd_glu_gelu_kernel(
         wrapped = w1_scales.rearrange("e s q n -> (e s q) n")[0:28, :].bitcast(I32)
         nc.scalar.dma_start(w1s_first[0][0:112, :].bitcast(I32), wrapped.unsqueeze(0).to_broadcast([4, 28, H // 4]))
         load_words(nc.sync, w3w, w3_words, 0, 1)
-        wrapped = w3_scales.rearrange("e s q n -> (e s q) n")[0:28, :].bitcast(I32)
-        nc.sync.dma_start(w3s_first[0:112, :].bitcast(I32), wrapped.unsqueeze(0).to_broadcast([4, 28, H // 4]))
+        load_scales(w3s, w3_scales, 0, E)
         load_words(nc.sync, w1w, w1_words, 1, 2)
         load_scales(w1s, w1_scales, 1, E)
         load_words(nc.sync, w3w, w3_words, 1, 2)
-        load_scales(w3s, w3_scales, 1, E)
         load_words(nc.sync, w1w, w1_words, 2, 4)
         load_words(nc.sync, w3w, w3_words, 2, 4)
         nc.sync.dma_start(pos1_sb[:], pos1)
@@ -135,7 +131,7 @@ def tile_moe_pkd_glu_gelu_kernel(
 
         def linear_side(j):
             b = psum.tile([P, H], F32, name="b", tag="bank%d" % (4, 5, 6, 7, 2, 3, 6, 7)[j])
-            product(b, j, w3w, [w3s_first[:]] + [w3s[:, e, :] for e in range(E - 1)])
+            product(b, j, w3w, [w3s[:, e, :] for e in range(E)])
             h = work.tile([P, H], BF16, name="h", align_bytes=64)
             if j < 2:
                 lin = work.tile([P, H], F32, name="lin", align_bytes=64)

from contextlib import ExitStack

import concourse.mybir as mybir
from concourse.masks import make_identity

K, T, E, C, H, N = 512, 512, 4, 256, 512, 128
P = 128
TAIL = 192
FLOPS = 2 * E * C * (2 * K * H + H * N)

F32 = mybir.dt.float32
BF16 = mybir.dt.bfloat16
I32 = mybir.dt.int32
U32 = mybir.dt.uint32
U16 = mybir.dt.uint16
U8 = mybir.dt.uint8
FP8X4 = mybir.dt.float8_e4m3fn_x4
FP4X4 = mybir.dt.float4_e2m1fn_x4
MULT = mybir.AluOpType.mult
ADD = mybir.AluOpType.add
GELU = mybir.ActivationFunctionType.Gelu_apprx_tanh
COPY = mybir.ActivationFunctionType.Copy


def tile_moe_pkd_glu_gelu_kernel(
    tc, x_words, x_scales, w1_words, w1_scales, w3_words, w3_scales, w2_words, w2_scales, gate, offs, pos1, pos2, out
):
    nc = tc.nc
    with ExitStack() as ctx:
        keep = ctx.enter_context(tc.tile_pool(name="keep", bufs=1))
        work = ctx.enter_context(tc.tile_pool(name="work", bufs=8))
        psum = ctx.enter_context(tc.psum_pool(name="psum", bufs=1))

        offs_sb = keep.tile([P, E * C // 16], U16, name="offs_sb")
        pos1_sb = keep.tile([P, T // 16], U16, name="pos1_sb")
        pos2_sb = keep.tile([P, T // 16], U16, name="pos2_sb")
        xw = keep.tile([P, T], U32, name="xw", tag="early_words", align_bytes=64)
        xs = keep.tile([P, T + TAIL], U8, name="xs", tag="early_scales", align_bytes=64)
        w1w = keep.tile([P, E, 2 * H], U8, name="w1w", align_bytes=64)
        w3w = keep.tile([P, E, 2 * H], U8, name="w3w", align_bytes=64)
        w1s_first = [keep.tile([P, H], U8, name="w1s_first%d" % e, align_bytes=64) for e in range(1)]
        w1s = keep.tile([P, E - 1, H], U8, name="w1s", align_bytes=64)
        w3s = keep.tile([P, E, H], U8, name="w3s", align_bytes=64)
        w2s = keep.tile([P, E, N], U8, name="w2s", align_bytes=64)
        w2w = keep.tile([P, E, 2 * N], U8, name="w2w", align_bytes=64)
        ident = keep.tile([P, P], F32, name="ident", align_bytes=64)
        ys = keep.tile([P, E * C], F32, name="ys", align_bytes=64)

        for plane in w1s_first:
            nc.vector.memset(plane[:].bitcast(I32), 0)
        for plane in (w3s, w1s):
            nc.vector.memset(plane[:].rearrange("p e n -> p (e n)").bitcast(I32), 0)
        nc.vector.memset(ident[:], 0.0)
        make_identity(nc, ident[:], nomemset=True)
        nc.vector.memset(w2s[:].rearrange("p e n -> p (e n)").bitcast(I32), 0)

        def load_words(queue, dst, src, e0, e1):
            queue.dma_start(dst[:, e0:e1, :].bitcast(I32), src[e0:e1, 0].bitcast(I32).rearrange("e p n -> p e n"))

        def load_scales(dst, src, e0, e1):
            for r in range(4):
                nc.sync.dma_start(
                    dst[r:P:32, :, :].bitcast(I32),
                    src[e0:e1, 0, r:16:4, :].rearrange("e q n -> q e n").bitcast(I32),
                )

        for q in range(4):
            rows = x_scales[0, 4 * q : 4 * q + 4, :].bitcast(I32)
            queue = nc.sync if q < 3 else nc.scalar
            queue.dma_start(xs[32 * q : 32 * q + 32, :T].bitcast(I32), rows.unsqueeze(0).to_broadcast([8, 4, T // 4]))
        nc.sync.dma_start(offs_sb[:], offs)
        nc.scalar.dma_start(xw[:].bitcast(I32), x_words[0].rearrange("p t r -> p (t r)").bitcast(I32))
        load_words(nc.scalar, w1w, w1_words, 0, 1)
        wrapped = w1_scales.rearrange("e s q n -> (e s q) n")[0:28, :].bitcast(I32)
        nc.scalar.dma_start(w1s_first[0][0:112, :].bitcast(I32), wrapped.unsqueeze(0).to_broadcast([4, 28, H // 4]))
        load_words(nc.sync, w3w, w3_words, 0, 1)
        load_scales(w3s, w3_scales, 0, E)
        load_words(nc.sync, w1w, w1_words, 1, 2)
        load_scales(w1s, w1_scales, 1, E)
        load_words(nc.sync, w3w, w3_words, 1, 2)
        load_words(nc.sync, w1w, w1_words, 2, 4)
        load_words(nc.sync, w3w, w3_words, 2, 4)
        nc.sync.dma_start(pos1_sb[:], pos1)
        nc.sync.dma_start(pos2_sb[:], pos2)

        gw = [keep.tile([P, C], U32, name="gw%d" % e, align_bytes=64) for e in range(E)]
        gs_late = keep.tile([P, 2 * C], U8, name="gs_late", align_bytes=64)
        gs = [keep.tile([P, C], U8, name="gs%d" % e, align_bytes=64) for e in range(2)]
        gs = gs + [gs_late[:, :C], gs_late[:, C:]]

        def gather(e, first, count):
            picks = offs_sb[:, (e * C + first) // 16 : (e * C + first + count) // 16]
            if e < 2:
                nc.vector.tensor_copy(gs[e][:, first : first + count], xs[:].indirect(picks))
            elif e == 2:
                nc.vector.tensor_copy(gs_late[:], xs[:].indirect(offs_sb[:, 2 * C // 16 :]))
            step = P if e == 0 else C
            for lo in range(0, C, step):
                picks = offs_sb[:, (e * C + lo) // 16 : (e * C + lo + step) // 16]
                nc.vector.tensor_copy(gw[e][:, lo : lo + step], xw[:].indirect(picks))

        nc.vector.memset(xs[:, T:].bitcast(I32), 0)
        load_scales(w2s, w2_scales, 0, E)
        load_words(nc.sync, w2w, w2_words, 0, 4)

        gelus, hs, hTs = {}, {}, {}

        def product(acc, j, ww, ws):
            e, cols = j // 2, slice((j % 2) * P, (j % 2 + 1) * P)
            nc.tensor.matmul_mx(
                out=acc[:],
                lhsT=gw[e][:, cols].bitcast(FP8X4),
                lhsT_scale=gs[e][:, cols],
                rhs=ww[:, e, :].bitcast(FP4X4),
                rhs_scale=ws[e],
                start=True,
                stop=True,
            )

        def gelu_side(j):
            a = psum.tile([P, H], F32, name="a", tag="bank%d" % (0, 1, 2, 3, 0, 1, 4, 5)[j])
            product(a, j, w1w, [t[:] for t in w1s_first] + [w1s[:, e, :] for e in range(E - 1)])
            if j < 7:
                g = work.tile([P, H], F32, name="g", align_bytes=64)
            else:
                g = keep.tile([P, H], F32, name="g_last", tag="last", align_bytes=64)
            nc.scalar.activation(
                g[:].rearrange("s (u p d) -> s u p d", u=2, d=2), a[:].rearrange("s (p u d) -> s u p d", u=2, d=2), GELU
            )
            gelus[j] = g

        def linear_side(j):
            b = psum.tile([P, H], F32, name="b", tag="bank%d" % (4, 5, 6, 7, 2, 3, 6, 7)[j])
            product(b, j, w3w, [w3s[:, e, :] for e in range(E)])
            h = work.tile([P, H], BF16, name="h", align_bytes=64)
            if j < 2:
                lin = work.tile([P, H], F32, name="lin", align_bytes=64)
                nc.scalar.copy(
                    lin[:].rearrange("s (u p d) -> s u p d", u=2, d=2), b[:].rearrange("s (p u d) -> s u p d", u=2, d=2)
                )
                nc.gpsimd.tensor_tensor(h[:], lin[:], gelus[j][:], MULT)
            else:
                nc.vector.tensor_tensor(
                    h[:].rearrange("s (u p d) -> s u p d", u=2, d=2),
                    b[:].rearrange("s (p u d) -> s u p d", u=2, d=2),
                    gelus[j][:].rearrange("s (u p d) -> s u p d", u=2, d=2),
                    MULT,
                )
            hs[j] = h

        def turn(tiles, bank):
            width = P * len(tiles)
            turned = psum.tile([P, 2, width], F32, name="turned", tag="bank%d" % bank)
            for n, j in enumerate(tiles):
                words = hs[j][:].bitcast(F32)
                for u in range(2):
                    nc.tensor.transpose(turned[:, u, n * P : (n + 1) * P], words[:, u * P : (u + 1) * P], ident[:])
            hT = work.tile([P, 4 * width], BF16, name="hT", align_bytes=64)
            nc.scalar.copy(hT[:].bitcast(F32).rearrange("p (s u) -> p s u", u=2), turned[:].rearrange("p u s -> p s u"))
            hTs[tiles] = hT

        def second_layer(tiles, bank):
            width = P * len(tiles)
            e = tiles[0] // 2
            hq = hq_all[:, tiles[0] * P : tiles[0] * P + width]
            hqs = work.tile([P, width], U8, name="hqs", align_bytes=64)
            nc.vector.quantize_mx(out=hq.bitcast(FP8X4), scales=hqs[:], in_=hTs[tiles][:])
            y = psum.tile([P, width], F32, name="y", tag="bank%d" % bank)
            nc.tensor.matmul_mx(
                out=y[:],
                lhsT=w2w[:, e, :].bitcast(FP4X4),
                lhsT_scale=w2s[:, e, :],
                rhs=hq.bitcast(FP8X4),
                rhs_scale=hqs[:],
                start=True,
                stop=True,
            )
            nc.scalar.copy(ys[:, tiles[0] * P : tiles[0] * P + width], y[:])

        for e in range(E):
            gather(e, 0, C)
        gate_sb = keep.tile([P, 2, T], F32, name="gate_sb", tag="early_scales", align_bytes=64)
        nc.sync.dma_start(gate_sb[:], gate.rearrange("g n t -> n g t"))
        for pair in ((0, 1), (2, 3)):
            for j in pair:
                gelu_side(j)
            for j in pair:
                linear_side(j)
        for j in range(4, 8):
            gelu_side(j)
        for j in range(4, 8):
            linear_side(j)
        groups = ((0, 1), (2, 3), (4, 5), (6,), (7,))
        for tiles, bank in zip(groups, (1, 4, 0, 5, 2)):
            turn(tiles, bank)
        hq_all = keep.tile([P, E * C], U32, name="hq_all", align_bytes=64)
        for tiles, bank in zip(groups, (3, 6, 1, 7, 4)):
            second_layer(tiles, bank)

        first = keep.tile([P, T], F32, name="first", align_bytes=64)
        second = keep.tile([P, T], F32, name="second", align_bytes=64)
        res = keep.tile([P, T], F32, name="res", align_bytes=64)
        halves = (slice(0, T // 2), slice(T // 2, T))
        nc.vector.tensor_tensor(first[:], ys[:].indirect(pos1_sb[:]), gate_sb[:, 0, :], MULT)
        picked = keep.tile([P, T], F32, name="picked", align_bytes=64)
        for half in halves:
            picks = pos2_sb[:, half.start // 16 : half.stop // 16]
            nc.scalar.activation(picked[:, half], ys[:].indirect(picks), COPY)
        for half in halves:
            nc.vector.tensor_tensor(second[:, half], picked[:, half], gate_sb[:, 1, half], MULT)
        for half in halves:
            nc.vector.tensor_tensor(res[:, half], first[:, half], second[:, half], ADD)
            nc.sync.dma_start(out[:, half], res[:, half])
